import numpy as np
CORES = [3,5,19,21,35,37,51,53,67,69]
N = 10
W = 256
def setup_inputs(rng):
    amp = 0.5 + 1.5 * rng.random((2, N, 128, 1), dtype=np.float32)
    return {"u": amp[0] * rng.standard_normal((N, 128, W), dtype=np.float32), "b": amp[1] * rng.standard_normal((N, 128, W), dtype=np.float32)}
def setup_inputs_big(rng):
    d = setup_inputs(rng)
    for k in ("u", "b"): d[k] = (d[k].astype(np.float32) * 1024.0).astype(d[k].dtype)
    return d
def setup_inputs_small(rng):
    d = setup_inputs(rng)
    for k in ("u", "b"): d[k] = (d[k].astype(np.float32) * (1 / 1024.0)).astype(d[k].dtype)
    return d
def setup_inputs_apart(rng):
    d = setup_inputs(rng)
    f = (10.0 ** rng.permutation(np.linspace(-1.5, 1.5, N))).astype(np.float32).reshape(N, 1, 1)
    for k in ("u", "b"): d[k] = (d[k].astype(np.float32) * f).astype(d[k].dtype)
    return d
def reference(u, b):
    g = np.concatenate(list(u.astype(np.float64)), axis=1); bb = np.concatenate(list(b.astype(np.float64)), axis=1)
    p = np.concatenate([g[:, -2:], g, g[:, :2]], axis=1)
    n = 0.125 * (p[:, :-4] + p[:, 1:-3] + p[:, 3:-1] + p[:, 4:]) + 0.5 * bb
    d = n - g
    s = np.stack([(d ** 2).mean(axis=1), np.abs(d).max(axis=1)], axis=1)
    return {"y": np.stack([n[:, W * r:W * r + W] for r in range(N)]).astype(np.float32), "s": np.broadcast_to(s.astype(np.float32), (N, 128, 2))}

@@ -1,0 +1,223 @@
+from concourse.bass import DstId, RemoteDMATransfer
+from concourse.mybir import AluOpType
+
+W = 256
+E = 32
+SCRATCH = {
+    "U": ("sbuf", [128, 264], "float32"),
+    "B": ("sbuf", [128, 256], "float32"),
+    "P": ("sbuf", [128, 260], "float32"),
+    "S": ("sbuf", [128, 256], "float32"),
+    "NE": ("sbuf", [128, 256], "float32"),
+    "ND": ("sbuf", [128, 256], "float32"),
+    "A": ("sbuf", [128, 256], "float32"),
+    "Q": ("sbuf", [128, 256], "float32"),
+    "TA": ("sbuf", [128, 128], "float32"),
+    "TQ": ("sbuf", [128, 128], "float32"),
+    "Y": ("sbuf", [128, 256], "float32"),
+    "L": ("sbuf", [128, 40], "float32"),
+    "RA": ("sbuf", [128, 40], "float32"),
+    "RQ": ("sbuf", [128, 40], "float32"),
+    "KC": ("sbuf", [128, 4], "float32"),
+    "SO": ("sbuf", [128, 2], "float32"),
+    "ps0": ("psum", [128, 512], "float32"),
+    "ps1": ("psum", [128, 512], "float32"),
+    "ps2": ("psum", [128, 512], "float32"),
+}
+SEMAPHORES = ["lu", "lb", "v", "halo", "pp", "red1", "red2", "sent", "pr", "yr", "sr", "st"]
+
+
+def _bits(m):
+    return bin(m).count("1")
+
+
+def _take(m, n):
+    out, k = 0, 0
+    while n > 0:
+        if (m >> k) & 1:
+            out |= 1 << k
+            n -= 1
+        k += 1
+    return out
+
+
+def rank_program(g, core, T, topo):
+    rank = T.rank_of(core)
+    if rank is None:
+        return
+    cores = list(T.cores)
+    n = len(cores)
+    sem = T.sem
+    V = g.vector
+    ADD, SUB, MUL, MAX = AluOpType.add, AluOpType.subtract, AluOpType.mult, AluOpType.max
+
+    chips = []
+    for c in cores:
+        if topo.chip(c) not in chips:
+            chips.append(topo.chip(c))
+    on_chip = {ch: sorted([c for c in cores if topo.chip(c) == ch], key=topo.die) for ch in chips}
+    nch = len(chips)
+    k = chips.index(topo.chip(core))
+    a = on_chip[chips[k]].index(core)
+    mate = on_chip[chips[k]][1 - a]
+
+    def tmask(src, dst):
+        if topo.chip(src) != topo.chip(dst):
+            return topo.mask(src, dst)
+        far_core = [c for c in cores if topo.chip(c) != topo.chip(src)][0]
+        return _take(topo.mask(src, dst) & ~topo.mask(src, far_core), 4)
+
+    def did(dst):
+        assert topo.may_write(core, dst)
+        rid, pid, _ = topo.addr(dst)
+        return DstId(rid=rid, pnc=pid)
+
+    U, B, P, S, NE, ND, A, Q, TA, TQ, Y, L, RA, RQ, KC, SO = (
+        T.U, T.B, T.P, T.S, T.NE, T.ND, T.A, T.Q, T.TA, T.TQ, T.Y, T.L, T.RA, T.RQ, T.KC, T.SO)
+    ps0, ps1, ps2 = T.ps0, T.ps1, T.ps2
+
+    def c2(lo, hi):
+        return ps0[:, lo:hi]
+
+    def c8(lo, hi):
+        return ps0[:, 256 + lo:256 + hi]
+
+    def hb(lo, hi):
+        return ps1[:, lo:hi]
+
+    def w(lo, hi):
+        return ps1[:, 256 + lo:256 + hi]
+
+    def d(lo, hi):
+        return ps2[:, lo:hi]
+
+    Ap, Qp, A1, Q1 = ps2[:, 256:320], ps2[:, 320:384], ps2[:, 384:448], ps2[:, 448:512]
+
+    g.sync.dma_start(out=U[:, 4:260], in_=T.u[:, :]).then_inc(sem.lu, 16)
+    g.scalar.dma_start(out=B[:, :], in_=T.b[:, :]).then_inc(sem.lb, 16)
+
+    cnt = [0]
+
+    def vwait():
+        if cnt[0]:
+            V.wait_ge(sem.v, cnt[0])
+
+    def done(ins, s):
+        if s is None:
+            ins.then_inc(sem.v, 1)
+            cnt[0] += 1
+        else:
+            ins.then_inc(s, 1)
+
+    def fill(ap, val):
+        done(V.memset(ap, val), None)
+
+    def tt(out, x, y, op, dep=True, s=None):
+        if dep:
+            vwait()
+        done(V.tensor_tensor(out=out, in0=x, in1=y, op=op), s)
+
+    own = 4 * a
+    fill(c2(0, 256), 0.5)
+    fill(c8(0, 256), 0.125)
+    fill(KC[:, :], -1.0 / (n * W))
+    fill(L[:, own + 2:own + 4], 0.0)
+
+    V.wait_ge(sem.lu, 16)
+    tt(P[:, E:W - E + 3], U[:, E + 2:W - E + 5], U[:, E + 3:W - E + 6], ADD)
+    tt(S[:, 2 * E:W], P[:, E:W - E], P[:, E + 3:W - E + 3], ADD)
+    V.wait_ge(sem.lb, 16)
+    tt(hb(0, E), B[:, W - E:W], c2(0, E), MUL, dep=False)
+    tt(hb(E, W), B[:, 0:W - E], c2(E, W), MUL, dep=False)
+    tt(NE[:, 0:E], U[:, 4 + W - E:4 + W], hb(0, E), SUB)
+    tt(NE[:, E:W], U[:, 4:4 + W - E], hb(E, W), SUB, dep=False)
+    tt(w(64, 256), S[:, 64:256], c8(64, 256), MUL, dep=False)
+    tt(d(64, 256), w(64, 256), NE[:, 64:256], SUB)
+    tt(ND[:, 64:256], NE[:, 64:256], w(64, 256), SUB, dep=False)
+    tt(Ap, d(64, 128), ND[:, 64:128], MAX)
+    tt(A[:, 128:256], d(128, 256), ND[:, 128:256], MAX, dep=False)
+    tt(Qp, d(64, 128), ND[:, 64:128], MUL, dep=False)
+    tt(Q[:, 128:256], d(128, 256), ND[:, 128:256], MUL, dep=False)
+    tt(A1, Ap, A[:, 128:192], MAX)
+    tt(Q1, Qp, Q[:, 128:192], ADD, dep=False)
+    tt(Ap, A1, A[:, 192:256], MAX)
+    tt(Qp, Q1, Q[:, 192:256], ADD, dep=False)
+
+    left, right = cores[(rank - 1) % n], cores[(rank + 1) % n]
+    V.wait_ge(sem.halo, _bits(tmask(left, core)) + _bits(tmask(right, core)))
+    tt(P[:, 0:E], U[:, 2:E + 2], U[:, 3:E + 3], ADD, dep=False)
+    tt(P[:, W - E + 3:W + 3], U[:, W - E + 5:W + 5], U[:, W - E + 6:W + 6], ADD, dep=False)
+    tt(S[:, 0:E], P[:, W - E:W], P[:, W - E + 3:W + 3], ADD)
+    tt(S[:, E:2 * E], P[:, 0:E], P[:, 3:E + 3], ADD, dep=False)
+    tt(w(0, 64), S[:, 0:64], c8(0, 64), MUL)
+    tt(d(0, 64), w(0, 64), NE[:, 0:64], SUB)
+    tt(ND[:, 0:64], NE[:, 0:64], w(0, 64), SUB, dep=False)
+    tt(A[:, 0:64], d(0, 64), ND[:, 0:64], MAX)
+    tt(Q[:, 0:64], d(0, 64), ND[:, 0:64], MUL, dep=False)
+    tt(TA[:, 0:64], Ap, A[:, 0:64], MAX)
+    tt(TQ[:, 0:64], Qp, Q[:, 0:64], ADD, dep=False)
+    o, wd = 0, 32
+    while wd >= 2:
+        tt(TA[:, o + 2 * wd:o + 3 * wd], TA[:, o:o + wd], TA[:, o + wd:o + 2 * wd], MAX)
+        tt(TQ[:, o + 2 * wd:o + 3 * wd], TQ[:, o:o + wd], TQ[:, o + wd:o + 2 * wd], ADD, dep=False)
+        o, wd = o + 2 * wd, wd // 2
+    tt(L[:, own:own + 1], TQ[:, o:o + 1], TQ[:, o + 1:o + 2], ADD)
+    tt(L[:, own + 1:own + 2], TA[:, o:o + 1], TA[:, o + 1:o + 2], MAX, s=sem.pr)
+
+    tt(Y[:, 0:W - E], U[:, 4:4 + W - E], d(E, W), ADD, dep=False)
+    tt(Y[:, W - E:W], U[:, 4 + W - E:4 + W], d(0, E), ADD, s=sem.yr)
+
+    g.wait_ge(sem.lu, 16)
+    g.remote_dma_fused([
+        RemoteDMATransfer(dst_ids=[did(left)], dma_engine_mask=tmask(core, left), remote_sem=sem.halo,
+                          srcs=[U[:, 4:6]], dsts=[U[:, 260:262]], alu_op=0),
+        RemoteDMATransfer(dst_ids=[did(right)], dma_engine_mask=tmask(core, right), remote_sem=sem.halo,
+                          srcs=[U[:, 258:260]], dsts=[U[:, 2:4]], alu_op=0),
+    ], local_sem=sem.sent)
+    nsent = _bits(tmask(core, left)) + _bits(tmask(core, right))
+
+    near = list(range(1, 1 + (nch - 1) // 2))
+    far = list(range(1 + (nch - 1) // 2, nch))
+    d1 = [(t, dl) for dl in near for t in on_chip[chips[(k + dl) % nch]]]
+    d2 = [(on_chip[chips[(k + dl) % nch]][a], dl) for dl in far]
+    m1, m2 = tmask(core, d1[0][0]), tmask(core, d2[0][0])
+    g.wait_ge(sem.pr, 1)
+    g.remote_dma_fused([
+        RemoteDMATransfer(dst_ids=[did(mate)], dma_engine_mask=tmask(core, mate), remote_sem=sem.pp,
+                          srcs=[L[:, own:own + 4]], dsts=[L[:, own:own + 4]], alu_op=0),
+        RemoteDMATransfer(dst_ids=[did(t) for t, dl in d1], dma_engine_mask=m1, remote_sem=sem.red1,
+                          srcs=[L[:, own:own + 4]], dsts=[L[:, 8 * dl + own:8 * dl + own + 4] for t, dl in d1],
+                          alu_op=0),
+    ], local_sem=sem.sent)
+    nsent += _bits(tmask(core, mate)) + _bits(m1)
+    g.wait_ge(sem.pp, _bits(tmask(mate, core)))
+    g.remote_dma_fused([
+        RemoteDMATransfer(dst_ids=[did(t) for t, dl in d2], dma_engine_mask=m2, remote_sem=sem.red2,
+                          srcs=[L[:, 0:8]], dsts=[L[:, 8 * dl:8 * dl + 8] for t, dl in d2], alu_op=0),
+    ], local_sem=sem.sent)
+    nsent += _bits(m2)
+    g.wait_ge(sem.sent, nsent)
+
+    n1 = sum(_bits(tmask(t, core)) for dl in near for t in on_chip[chips[(k - dl) % nch]])
+    n2 = sum(_bits(tmask(on_chip[chips[(k - dl) % nch]][a], core)) for dl in far)
+    V.wait_ge(sem.pr, 1)
+    V.wait_ge(sem.pp, _bits(tmask(mate, core)))
+    V.wait_ge(sem.red1, n1)
+    tt(RQ[:, 0:8], L[:, 0:8], L[:, 8:16], ADD, dep=False)
+    tt(RA[:, 0:8], L[:, 0:8], L[:, 8:16], MAX, dep=False)
+    tt(RQ[:, 8:16], RQ[:, 0:8], L[:, 16:24], ADD)
+    tt(RA[:, 8:16], RA[:, 0:8], L[:, 16:24], MAX, dep=False)
+    V.wait_ge(sem.red2, n2)
+    tt(RQ[:, 16:24], L[:, 24:32], L[:, 32:40], ADD, dep=False)
+    tt(RA[:, 16:24], L[:, 24:32], L[:, 32:40], MAX, dep=False)
+    tt(RQ[:, 24:32], RQ[:, 16:24], RQ[:, 8:16], ADD)
+    tt(RA[:, 24:32], RA[:, 16:24], RA[:, 8:16], MAX, dep=False)
+    tt(RQ[:, 32:33], RQ[:, 24:25], RQ[:, 28:29], ADD)
+    tt(SO[:, 1:2], RA[:, 25:26], RA[:, 29:30], MAX, dep=False)
+    tt(SO[:, 0:1], RQ[:, 32:33], KC[:, 0:1], MUL, s=sem.sr)
+
+    g.sync.wait_ge(sem.yr, 1)
+    g.sync.dma_start(out=T.y[:, :], in_=Y[:, :]).then_inc(sem.st, 16)
+    g.sync.wait_ge(sem.sr, 1)
+    g.sync.dma_start(out=T.s[:, :], in_=SO[:, :]).then_inc(sem.st, 16)
+    g.sync.wait_ge(sem.st, 32)

@@ -1,30 +1,39 @@
+import math
 from concourse.bass import DstId, RemoteDMATransfer
-from concourse.mybir import AluOpType
+from concourse.mybir import AluOpType, AxisListType, ActivationFunctionType
 
 W = 256
-E = 32
+BL = 12
+SH = BL + 6
 SCRATCH = {
     "U": ("sbuf", [128, 264], "float32"),
     "B": ("sbuf", [128, 256], "float32"),
-    "P": ("sbuf", [128, 260], "float32"),
-    "S": ("sbuf", [128, 256], "float32"),
-    "NE": ("sbuf", [128, 256], "float32"),
-    "ND": ("sbuf", [128, 256], "float32"),
-    "A": ("sbuf", [128, 256], "float32"),
-    "Q": ("sbuf", [128, 256], "float32"),
-    "TA": ("sbuf", [128, 128], "float32"),
-    "TQ": ("sbuf", [128, 128], "float32"),
+    "U8": ("sbuf", [128, 256], "float32"),
+    "P": ("sbuf", [128, 264], "float32"),
+    "F": ("sbuf", [128, 260], "float32"),
+    "G": ("sbuf", [128, 260], "float32"),
+    "SQ": ("sbuf", [128, 256], "float32"),
+    "SQ2": ("sbuf", [128, 64], "float32"),
+    "SQ3": ("sbuf", [128, 64], "float32"),
     "Y": ("sbuf", [128, 256], "float32"),
-    "L": ("sbuf", [128, 40], "float32"),
-    "RA": ("sbuf", [128, 40], "float32"),
-    "RQ": ("sbuf", [128, 40], "float32"),
-    "KC": ("sbuf", [128, 4], "float32"),
+    "HB": ("sbuf", [128, 8], "float32"),
+    "HC": ("sbuf", [128, 4], "float32"),
+    "L": ("sbuf", [128, 132], "float32"),
+    "E": ("sbuf", [128, 128], "float32"),
+    "EB": ("sbuf", [128, 64], "float32"),
+    "EM": ("sbuf", [128, 64], "float32"),
+    "EB2": ("sbuf", [128, 64], "float32"),
+    "EM2": ("sbuf", [128, 64], "float32"),
+    "QS": ("sbuf", [128, 4], "float32"),
     "SO": ("sbuf", [128, 2], "float32"),
-    "ps0": ("psum", [128, 512], "float32"),
-    "ps1": ("psum", [128, 512], "float32"),
-    "ps2": ("psum", [128, 512], "float32"),
+    "psB": ("psum", [128, 512], "float32"),
+    "psP": ("psum", [128, 512], "float32"),
+    "psS": ("psum", [128, 512], "float32"),
+    "psY": ("psum", [128, 512], "float32"),
+    "psM": ("psum", [128, 512], "float32"),
 }
-SEMAPHORES = ["lu", "lb", "v", "halo", "pp", "red1", "red2", "sent", "pr", "yr", "sr", "st"]
+SEMAPHORES = ["lu", "lb", "mz", "v", "ab", "pd", "ap", "gd", "pr", "halo", "ge", "ay", "yr", "pp", "red1", "red2",
+              "sent", "eb", "ae", "fb", "af", "sr", "st"]
 
 
 def _bits(m):
@@ -48,18 +57,24 @@ def rank_program(g, core, T, topo):
     cores = list(T.cores)
     n = len(cores)
     sem = T.sem
-    V = g.vector
+    V, ACT = g.vector, g.scalar
     ADD, SUB, MUL, MAX = AluOpType.add, AluOpType.subtract, AluOpType.mult, AluOpType.max
+    COPY, SQUARE = ActivationFunctionType.Copy, ActivationFunctionType.Square
+    X = AxisListType.X
 
     chips = []
     for c in cores:
         if topo.chip(c) not in chips:
             chips.append(topo.chip(c))
-    on_chip = {ch: sorted([c for c in cores if topo.chip(c) == ch], key=topo.die) for ch in chips}
+    on_chip = {ch: [c for c in cores if topo.chip(c) == ch] for ch in chips}
     nch = len(chips)
     k = chips.index(topo.chip(core))
     a = on_chip[chips[k]].index(core)
     mate = on_chip[chips[k]][1 - a]
+    CH = 2 * BL
+
+    def same_die(ch, c):
+        return [t for t in on_chip[ch] if topo.die(t) == topo.die(c)][0]
 
     def tmask(src, dst):
         if topo.chip(src) != topo.chip(dst):
@@ -72,29 +87,26 @@ def rank_program(g, core, T, topo):
         rid, pid, _ = topo.addr(dst)
         return DstId(rid=rid, pnc=pid)
 
-    U, B, P, S, NE, ND, A, Q, TA, TQ, Y, L, RA, RQ, KC, SO = (
-        T.U, T.B, T.P, T.S, T.NE, T.ND, T.A, T.Q, T.TA, T.TQ, T.Y, T.L, T.RA, T.RQ, T.KC, T.SO)
-    ps0, ps1, ps2 = T.ps0, T.ps1, T.ps2
+    U, B, U8, P, F, G, Y, HB, HC, L, E, QS, SO = (
+        T.U, T.B, T.U8, T.P, T.F, T.G, T.Y, T.HB, T.HC, T.L, T.E, T.QS, T.SO)
+    psB, psP, psS, psY, psM = T.psB, T.psP, T.psS, T.psY, T.psM
 
-    def c2(lo, hi):
-        return ps0[:, lo:hi]
+    def Mb(lo, hi):
+        return psM[:, lo:hi]
 
-    def c8(lo, hi):
-        return ps0[:, 256 + lo:256 + hi]
+    def M1(lo, hi):
+        return psM[:, 128 + lo:128 + hi]
 
-    def hb(lo, hi):
-        return ps1[:, lo:hi]
-
-    def w(lo, hi):
-        return ps1[:, 256 + lo:256 + hi]
-
-    def d(lo, hi):
-        return ps2[:, lo:hi]
-
-    Ap, Qp, A1, Q1 = ps2[:, 256:320], ps2[:, 320:384], ps2[:, 384:448], ps2[:, 448:512]
+    own = BL * a
+    sc = 1.0 / math.sqrt(64.0 * n * W)
+    near = list(range(1, 1 + (nch - 1) // 2))
+    far = list(range(1 + (nch - 1) // 2, nch))
+    jl = 2 * len(far) + 1
+    lo_l, hi_l = BL, BL * jl + 6
+    lo_e, hi_e = BL * (jl + 1), BL * n + 6
 
     g.sync.dma_start(out=U[:, 4:260], in_=T.u[:, :]).then_inc(sem.lu, 16)
-    g.scalar.dma_start(out=B[:, :], in_=T.b[:, :]).then_inc(sem.lb, 16)
+    ACT.dma_start(out=B[:, :], in_=T.b[:, :]).then_inc(sem.lb, 16)
 
     cnt = [0]
 
@@ -109,112 +121,137 @@ def rank_program(g, core, T, topo):
         else:
             ins.then_inc(s, 1)
 
-    def fill(ap, val):
-        done(V.memset(ap, val), None)
+    def fill(ap, val, s=None):
+        done(V.memset(ap, val), s)
 
     def tt(out, x, y, op, dep=True, s=None):
         if dep:
             vwait()
         done(V.tensor_tensor(out=out, in0=x, in1=y, op=op), s)
 
-    own = 4 * a
-    fill(c2(0, 256), 0.5)
-    fill(c8(0, 256), 0.125)
-    fill(KC[:, :], -1.0 / (n * W))
-    fill(L[:, own + 2:own + 4], 0.0)
+    def cp(out, x, dep=True, s=None):
+        if dep:
+            vwait()
+        done(V.tensor_copy(out=out, in_=x), s)
+
+    def red(out, x, op, ab=False, dep=True, s=None):
+        if dep:
+            vwait()
+        done(V.tensor_reduce(out=out, in_=x, axis=X, op=op, apply_absolute_value=ab), s)
+
+    fill(U[:, 0:4], 0.0, s=sem.mz)
+    fill(U[:, 260:264], 0.0, s=sem.mz)
+    fill(F[:, 0:2], 0.0)
+    fill(F[:, 258:260], 0.0)
+    fill(L[:, own + 10:own + 12], 0.0)
+
+    ACT.wait_ge(sem.lb, 16)
+    ACT.activation(out=psB[:, 0:W], in_=B[:, :], func=COPY, scale=4.0).then_inc(sem.ab, 1)
+    ACT.wait_ge(sem.lu, 16)
+    ACT.activation(out=U8[:, :], in_=U[:, 4:260], func=COPY, scale=8.0).then_inc(sem.ab, 1)
+    ACT.wait_ge(sem.pd, 1)
+    ACT.activation(out=psP[:, 0:263], in_=P[:, 0:263], func=COPY).then_inc(sem.ap, 1)
+    ACT.wait_ge(sem.gd, 1)
+    ACT.activation(out=L[:, own + 6:own + 10], in_=G[:, 0:4], func=COPY).then_inc(sem.pr, 1)
+    ACT.activation(out=T.SQ[:, 0:252], in_=G[:, 4:256], func=SQUARE, scale=sc,
+                   accum_out=L[:, own + 4:own + 5]).then_inc(sem.pr, 1)
 
     V.wait_ge(sem.lu, 16)
-    tt(P[:, E:W - E + 3], U[:, E + 2:W - E + 5], U[:, E + 3:W - E + 6], ADD)
-    tt(S[:, 2 * E:W], P[:, E:W - E], P[:, E + 3:W - E + 3], ADD)
-    V.wait_ge(sem.lb, 16)
-    tt(hb(0, E), B[:, W - E:W], c2(0, E), MUL, dep=False)
-    tt(hb(E, W), B[:, 0:W - E], c2(E, W), MUL, dep=False)
-    tt(NE[:, 0:E], U[:, 4 + W - E:4 + W], hb(0, E), SUB)
-    tt(NE[:, E:W], U[:, 4:4 + W - E], hb(E, W), SUB, dep=False)
-    tt(w(64, 256), S[:, 64:256], c8(64, 256), MUL, dep=False)
-    tt(d(64, 256), w(64, 256), NE[:, 64:256], SUB)
-    tt(ND[:, 64:256], NE[:, 64:256], w(64, 256), SUB, dep=False)
-    tt(Ap, d(64, 128), ND[:, 64:128], MAX)
-    tt(A[:, 128:256], d(128, 256), ND[:, 128:256], MAX, dep=False)
-    tt(Qp, d(64, 128), ND[:, 64:128], MUL, dep=False)
-    tt(Q[:, 128:256], d(128, 256), ND[:, 128:256], MUL, dep=False)
-    tt(A1, Ap, A[:, 128:192], MAX)
-    tt(Q1, Qp, Q[:, 128:192], ADD, dep=False)
-    tt(Ap, A1, A[:, 192:256], MAX)
-    tt(Qp, Q1, Q[:, 192:256], ADD, dep=False)
+    V.wait_ge(sem.mz, 2)
+    tt(P[:, 0:263], U[:, 0:263], U[:, 1:264], ADD, dep=False, s=sem.pd)
+    V.wait_ge(sem.ab, 2)
+    tt(F[:, 2:258], psB[:, 0:W], U8[:, :], SUB, dep=False)
+    V.wait_ge(sem.pd, 1)
+    V.wait_ge(sem.ap, 1)
+    tt(psS[:, 0:260], psP[:, 0:260], P[:, 3:263], ADD, dep=False)
+    tt(G[:, 0:260], psS[:, 0:260], F[:, 0:260], ADD, s=sem.gd)
+    V.wait_ge(sem.gd, 1)
+    red(L[:, own + 5:own + 6], G[:, 4:256], MAX, ab=True, dep=False, s=sem.pr)
+    cp(L[:, own:own + 4], G[:, 256:260], dep=False, s=sem.pr)
+
+    fill(psM[:, 0:256], 0.0)
+    fill(E[:, hi_l:hi_l + 6], 0.0)
+    fill(E[:, lo_e + BL * (n - jl - 1) - 6:lo_e + BL * (n - jl - 1)], 0.0)
+    vwait()
+    for m in range(4):
+        fill(psM[:, m:hi_e:BL], sc)
+        fill(psM[:, 128 + m:128 + hi_e:BL], 0.125)
+    fill(psM[:, 128 + 5:128 + hi_e:BL], 0.125)
+    fill(psM[:, 128 + hi_l:128 + hi_l + 1], 1.0)
 
     left, right = cores[(rank - 1) % n], cores[(rank + 1) % n]
+    V.wait_ge(sem.pr, 4)
     V.wait_ge(sem.halo, _bits(tmask(left, core)) + _bits(tmask(right, core)))
-    tt(P[:, 0:E], U[:, 2:E + 2], U[:, 3:E + 3], ADD, dep=False)
-    tt(P[:, W - E + 3:W + 3], U[:, W - E + 5:W + 5], U[:, W - E + 6:W + 6], ADD, dep=False)
-    tt(S[:, 0:E], P[:, W - E:W], P[:, W - E + 3:W + 3], ADD)
-    tt(S[:, E:2 * E], P[:, 0:E], P[:, 3:E + 3], ADD, dep=False)
-    tt(w(0, 64), S[:, 0:64], c8(0, 64), MUL)
-    tt(d(0, 64), w(0, 64), NE[:, 0:64], SUB)
-    tt(ND[:, 0:64], NE[:, 0:64], w(0, 64), SUB, dep=False)
-    tt(A[:, 0:64], d(0, 64), ND[:, 0:64], MAX)
-    tt(Q[:, 0:64], d(0, 64), ND[:, 0:64], MUL, dep=False)
-    tt(TA[:, 0:64], Ap, A[:, 0:64], MAX)
-    tt(TQ[:, 0:64], Qp, Q[:, 0:64], ADD, dep=False)
-    o, wd = 0, 32
-    while wd >= 2:
-        tt(TA[:, o + 2 * wd:o + 3 * wd], TA[:, o:o + wd], TA[:, o + wd:o + 2 * wd], MAX)
-        tt(TQ[:, o + 2 * wd:o + 3 * wd], TQ[:, o:o + wd], TQ[:, o + wd:o + 2 * wd], ADD, dep=False)
-        o, wd = o + 2 * wd, wd // 2
-    tt(L[:, own:own + 1], TQ[:, o:o + 1], TQ[:, o + 1:o + 2], ADD)
-    tt(L[:, own + 1:own + 2], TA[:, o:o + 1], TA[:, o + 1:o + 2], MAX, s=sem.pr)
-
-    tt(Y[:, 0:W - E], U[:, 4:4 + W - E], d(E, W), ADD, dep=False)
-    tt(Y[:, W - E:W], U[:, 4 + W - E:4 + W], d(0, E), ADD, s=sem.yr)
+    tt(HC[:, 0:2], HB[:, 0:2], HB[:, 1:3], ADD, dep=False)
+    tt(HC[:, 2:4], HB[:, 5:7], HB[:, 6:8], ADD, dep=False)
+    tt(G[:, 2:4], G[:, 2:4], HC[:, 0:2], ADD, s=sem.ge)
+    tt(G[:, 256:258], G[:, 256:258], HC[:, 2:4], ADD, dep=False, s=sem.ge)
+    ACT.wait_ge(sem.ge, 2)
+    ACT.activation(out=psY[:, 0:W], in_=G[:, 2:258], func=COPY, scale=0.125).then_inc(sem.ay, 1)
+    V.wait_ge(sem.ay, 1)
+    tt(Y[:, :], psY[:, 0:W], U[:, 4:260], ADD, dep=False, s=sem.yr)
 
     g.wait_ge(sem.lu, 16)
+    g.wait_ge(sem.mz, 2)
     g.remote_dma_fused([
         RemoteDMATransfer(dst_ids=[did(left)], dma_engine_mask=tmask(core, left), remote_sem=sem.halo,
-                          srcs=[U[:, 4:6]], dsts=[U[:, 260:262]], alu_op=0),
+                          srcs=[U[:, 2:6]], dsts=[HB[:, 4:8]], alu_op=0),
         RemoteDMATransfer(dst_ids=[did(right)], dma_engine_mask=tmask(core, right), remote_sem=sem.halo,
-                          srcs=[U[:, 258:260]], dsts=[U[:, 2:4]], alu_op=0),
+                          srcs=[U[:, 258:262]], dsts=[HB[:, 0:4]], alu_op=0),
     ], local_sem=sem.sent)
     nsent = _bits(tmask(core, left)) + _bits(tmask(core, right))
 
-    near = list(range(1, 1 + (nch - 1) // 2))
-    far = list(range(1 + (nch - 1) // 2, nch))
-    d1 = [(t, dl) for dl in near for t in on_chip[chips[(k + dl) % nch]]]
-    d2 = [(on_chip[chips[(k + dl) % nch]][a], dl) for dl in far]
+    d1 = [(t, nch - dl) for dl in near for t in on_chip[chips[(k + dl) % nch]]]
+    d2 = [(same_die(chips[(k + dl) % nch], core), nch - dl) for dl in far]
     m1, m2 = tmask(core, d1[0][0]), tmask(core, d2[0][0])
-    g.wait_ge(sem.pr, 1)
+    g.wait_ge(sem.pr, 4)
     g.remote_dma_fused([
         RemoteDMATransfer(dst_ids=[did(mate)], dma_engine_mask=tmask(core, mate), remote_sem=sem.pp,
-                          srcs=[L[:, own:own + 4]], dsts=[L[:, own:own + 4]], alu_op=0),
-        RemoteDMATransfer(dst_ids=[did(t) for t, dl in d1], dma_engine_mask=m1, remote_sem=sem.red1,
-                          srcs=[L[:, own:own + 4]], dsts=[L[:, 8 * dl + own:8 * dl + own + 4] for t, dl in d1],
+                          srcs=[L[:, own:own + BL]], dsts=[L[:, own:own + BL]], alu_op=0),
+        RemoteDMATransfer(dst_ids=[did(t) for t, sl in d1], dma_engine_mask=m1, remote_sem=sem.red1,
+                          srcs=[L[:, own:own + BL]], dsts=[L[:, CH * sl + own:CH * sl + own + BL] for t, sl in d1],
                           alu_op=0),
     ], local_sem=sem.sent)
     nsent += _bits(tmask(core, mate)) + _bits(m1)
     g.wait_ge(sem.pp, _bits(tmask(mate, core)))
     g.remote_dma_fused([
-        RemoteDMATransfer(dst_ids=[did(t) for t, dl in d2], dma_engine_mask=m2, remote_sem=sem.red2,
-                          srcs=[L[:, 0:8]], dsts=[L[:, 8 * dl:8 * dl + 8] for t, dl in d2], alu_op=0),
+        RemoteDMATransfer(dst_ids=[did(t) for t, sl in d2], dma_engine_mask=m2, remote_sem=sem.red2,
+                          srcs=[L[:, 0:CH]], dsts=[L[:, CH * sl:CH * sl + CH] for t, sl in d2], alu_op=0),
     ], local_sem=sem.sent)
     nsent += _bits(m2)
     g.wait_ge(sem.sent, nsent)
 
     n1 = sum(_bits(tmask(t, core)) for dl in near for t in on_chip[chips[(k - dl) % nch]])
-    n2 = sum(_bits(tmask(on_chip[chips[(k - dl) % nch]][a], core)) for dl in far)
-    V.wait_ge(sem.pr, 1)
+    n2 = sum(_bits(tmask(same_die(chips[(k - dl) % nch], core), core)) for dl in far)
+    we = hi_e - lo_e
     V.wait_ge(sem.pp, _bits(tmask(mate, core)))
     V.wait_ge(sem.red1, n1)
-    tt(RQ[:, 0:8], L[:, 0:8], L[:, 8:16], ADD, dep=False)
-    tt(RA[:, 0:8], L[:, 0:8], L[:, 8:16], MAX, dep=False)
-    tt(RQ[:, 8:16], RQ[:, 0:8], L[:, 16:24], ADD)
-    tt(RA[:, 8:16], RA[:, 0:8], L[:, 16:24], MAX, dep=False)
+    cp(L[:, BL * n:BL * n + BL], L[:, 0:BL], dep=False)
+    tt(E[:, BL * n:hi_e], L[:, 0:6], L[:, SH:SH + 6], ADD, dep=False)
+    tt(E[:, lo_e:BL * n - 6], L[:, lo_e:BL * n - 6], L[:, lo_e + SH:BL * n - 6 + SH], ADD)
+    tt(T.EB2[:, 0:we], E[:, lo_e:hi_e], Mb(lo_e, hi_e), MUL, s=sem.eb)
+    tt(T.EM2[:, 0:we], E[:, lo_e:hi_e], M1(lo_e, hi_e), MUL, dep=False)
+    red(QS[:, 0:1], E[:, lo_e + 4:hi_e:BL], ADD, dep=False)
+    ACT.wait_ge(sem.eb, 1)
+    ACT.activation(out=T.SQ2[:, 0:we], in_=T.EB2[:, 0:we], func=SQUARE,
+                   accum_out=QS[:, 1:2]).then_inc(sem.ae, 1)
+    red(E[:, hi_l:hi_l + 1], T.EM2[:, 0:we], MAX, ab=True)
+    V.wait_ge(sem.eb, 1)
+    V.wait_ge(sem.ae, 1)
+    tt(E[:, lo_e + 4:lo_e + 5], QS[:, 0:1], QS[:, 1:2], ADD)
+
+    wl = hi_l - lo_l
     V.wait_ge(sem.red2, n2)
-    tt(RQ[:, 16:24], L[:, 24:32], L[:, 32:40], ADD, dep=False)
-    tt(RA[:, 16:24], L[:, 24:32], L[:, 32:40], MAX, dep=False)
-    tt(RQ[:, 24:32], RQ[:, 16:24], RQ[:, 8:16], ADD)
-    tt(RA[:, 24:32], RA[:, 16:24], RA[:, 8:16], MAX, dep=False)
-    tt(RQ[:, 32:33], RQ[:, 24:25], RQ[:, 28:29], ADD)
-    tt(SO[:, 1:2], RA[:, 25:26], RA[:, 29:30], MAX, dep=False)
-    tt(SO[:, 0:1], RQ[:, 32:33], KC[:, 0:1], MUL, s=sem.sr)
+    tt(E[:, lo_l:hi_l], L[:, lo_l:hi_l], L[:, lo_l + SH:hi_l + SH], ADD, dep=False)
+    tt(T.EB[:, 0:wl], E[:, lo_l:hi_l], Mb(lo_l, hi_l), MUL, s=sem.fb)
+    tt(T.EM[:, 0:wl + 6], E[:, lo_l:hi_l + 6], M1(lo_l, hi_l + 6), MUL, dep=False)
+    red(QS[:, 2:3], E[:, lo_l + 4:lo_e + 5:BL], ADD, dep=False)
+    ACT.wait_ge(sem.fb, 1)
+    ACT.activation(out=T.SQ3[:, 0:wl], in_=T.EB[:, 0:wl], func=SQUARE,
+                   accum_out=QS[:, 3:4]).then_inc(sem.af, 1)
+    red(SO[:, 1:2], T.EM[:, 0:wl + 6], MAX, ab=True)
+    V.wait_ge(sem.af, 1)
+    tt(SO[:, 0:1], QS[:, 2:3], QS[:, 3:4], ADD, s=sem.sr)
 
     g.sync.wait_ge(sem.yr, 1)
     g.sync.dma_start(out=T.y[:, :], in_=Y[:, :]).then_inc(sem.st, 16)

@@ -6,11 +6,10 @@ W = 256
 BL = 12
 SH = BL + 6
 SCRATCH = {
-    "U": ("sbuf", [128, 264], "float32"),
+    "U": ("sbuf", [128, 272], "float32"),
     "B": ("sbuf", [128, 256], "float32"),
-    "U8": ("sbuf", [128, 256], "float32"),
-    "P": ("sbuf", [128, 264], "float32"),
-    "F": ("sbuf", [128, 260], "float32"),
+    "U9": ("sbuf", [128, 260], "float32"),
+    "B4": ("sbuf", [128, 260], "float32"),
     "G": ("sbuf", [128, 260], "float32"),
     "SQ": ("sbuf", [128, 256], "float32"),
     "SQ2": ("sbuf", [128, 64], "float32"),
@@ -26,9 +25,8 @@ SCRATCH = {
     "EM2": ("sbuf", [128, 64], "float32"),
     "QS": ("sbuf", [128, 4], "float32"),
     "SO": ("sbuf", [128, 2], "float32"),
-    "psB": ("psum", [128, 512], "float32"),
-    "psP": ("psum", [128, 512], "float32"),
-    "psS": ("psum", [128, 512], "float32"),
+    "psW": ("psum", [128, 512], "float32"),
+    "psH": ("psum", [128, 512], "float32"),
     "psY": ("psum", [128, 512], "float32"),
     "psM": ("psum", [128, 512], "float32"),
 }
@@ -87,9 +85,9 @@ def rank_program(g, core, T, topo):
         rid, pid, _ = topo.addr(dst)
         return DstId(rid=rid, pnc=pid)
 
-    U, B, U8, P, F, G, Y, HB, HC, L, E, QS, SO = (
-        T.U, T.B, T.U8, T.P, T.F, T.G, T.Y, T.HB, T.HC, T.L, T.E, T.QS, T.SO)
-    psB, psP, psS, psY, psM = T.psB, T.psP, T.psS, T.psY, T.psM
+    U, B, U9, B4, G, Y, HB, HC, L, E, QS, SO = (
+        T.U, T.B, T.U9, T.B4, T.G, T.Y, T.HB, T.HC, T.L, T.E, T.QS, T.SO)
+    psW, psH, psY, psM = T.psW, T.psH, T.psY, T.psM
 
     def Mb(lo, hi):
         return psM[:, lo:hi]
@@ -105,7 +103,7 @@ def rank_program(g, core, T, topo):
     lo_l, hi_l = BL, BL * jl + 6
     lo_e, hi_e = BL * (jl + 1), BL * n + 6
 
-    g.sync.dma_start(out=U[:, 4:260], in_=T.u[:, :]).then_inc(sem.lu, 16)
+    g.sync.dma_start(out=U[:, 8:264], in_=T.u[:, :]).then_inc(sem.lu, 16)
     ACT.dma_start(out=B[:, :], in_=T.b[:, :]).then_inc(sem.lb, 16)
 
     cnt = [0]
@@ -139,18 +137,17 @@ def rank_program(g, core, T, topo):
             vwait()
         done(V.tensor_reduce(out=out, in_=x, axis=X, op=op, apply_absolute_value=ab), s)
 
-    fill(U[:, 0:4], 0.0, s=sem.mz)
-    fill(U[:, 260:264], 0.0, s=sem.mz)
-    fill(F[:, 0:2], 0.0)
-    fill(F[:, 258:260], 0.0)
+    fill(U[:, 0:8], 0.0, s=sem.mz)
+    fill(U[:, 264:272], 0.0, s=sem.mz)
+    fill(B4[:, 0:2], 0.0)
+    fill(B4[:, 258:260], 0.0)
     fill(L[:, own + 10:own + 12], 0.0)
 
-    ACT.wait_ge(sem.lb, 16)
-    ACT.activation(out=psB[:, 0:W], in_=B[:, :], func=COPY, scale=4.0).then_inc(sem.ab, 1)
     ACT.wait_ge(sem.lu, 16)
-    ACT.activation(out=U8[:, :], in_=U[:, 4:260], func=COPY, scale=8.0).then_inc(sem.ab, 1)
-    ACT.wait_ge(sem.pd, 1)
-    ACT.activation(out=psP[:, 0:263], in_=P[:, 0:263], func=COPY).then_inc(sem.ap, 1)
+    ACT.wait_ge(sem.mz, 2)
+    ACT.activation(out=U9[:, :], in_=U[:, 6:266], func=COPY, scale=9.0).then_inc(sem.ap, 1)
+    ACT.wait_ge(sem.lb, 16)
+    ACT.activation(out=B4[:, 2:258], in_=B[:, :], func=COPY, scale=4.0).then_inc(sem.ab, 1)
     ACT.wait_ge(sem.gd, 1)
     ACT.activation(out=L[:, own + 6:own + 10], in_=G[:, 0:4], func=COPY).then_inc(sem.pr, 1)
     ACT.activation(out=T.SQ[:, 0:252], in_=G[:, 4:256], func=SQUARE, scale=sc,
@@ -158,13 +155,13 @@ def rank_program(g, core, T, topo):
 
     V.wait_ge(sem.lu, 16)
     V.wait_ge(sem.mz, 2)
-    tt(P[:, 0:263], U[:, 0:263], U[:, 1:264], ADD, dep=False, s=sem.pd)
-    V.wait_ge(sem.ab, 2)
-    tt(F[:, 2:258], psB[:, 0:W], U8[:, :], SUB, dep=False)
+    V.tensor_tensor_scan(out=psW[:, 0:260], data0=U[:, 8:268], data1=U[:, 3:263], initial=0.0,
+                         op0=ADD, op1=SUB).then_inc(sem.pd, 1)
     V.wait_ge(sem.pd, 1)
     V.wait_ge(sem.ap, 1)
-    tt(psS[:, 0:260], psP[:, 0:260], P[:, 3:263], ADD, dep=False)
-    tt(G[:, 0:260], psS[:, 0:260], F[:, 0:260], ADD, s=sem.gd)
+    tt(psH[:, 0:260], psW[:, 0:260], U9[:, :], SUB, dep=False)
+    V.wait_ge(sem.ab, 1)
+    tt(G[:, 0:260], psH[:, 0:260], B4[:, :], ADD, s=sem.gd)
     V.wait_ge(sem.gd, 1)
     red(L[:, own + 5:own + 6], G[:, 4:256], MAX, ab=True, dep=False, s=sem.pr)
     cp(L[:, own:own + 4], G[:, 256:260], dep=False, s=sem.pr)
@@ -189,15 +186,15 @@ def rank_program(g, core, T, topo):
     ACT.wait_ge(sem.ge, 2)
     ACT.activation(out=psY[:, 0:W], in_=G[:, 2:258], func=COPY, scale=0.125).then_inc(sem.ay, 1)
     V.wait_ge(sem.ay, 1)
-    tt(Y[:, :], psY[:, 0:W], U[:, 4:260], ADD, dep=False, s=sem.yr)
+    tt(Y[:, :], psY[:, 0:W], U[:, 8:264], ADD, dep=False, s=sem.yr)
 
     g.wait_ge(sem.lu, 16)
     g.wait_ge(sem.mz, 2)
     g.remote_dma_fused([
         RemoteDMATransfer(dst_ids=[did(left)], dma_engine_mask=tmask(core, left), remote_sem=sem.halo,
-                          srcs=[U[:, 2:6]], dsts=[HB[:, 4:8]], alu_op=0),
+                          srcs=[U[:, 6:10]], dsts=[HB[:, 4:8]], alu_op=0),
         RemoteDMATransfer(dst_ids=[did(right)], dma_engine_mask=tmask(core, right), remote_sem=sem.halo,
-                          srcs=[U[:, 258:262]], dsts=[HB[:, 0:4]], alu_op=0),
+                          srcs=[U[:, 262:266]], dsts=[HB[:, 0:4]], alu_op=0),
     ], local_sem=sem.sent)
     nsent = _bits(tmask(core, left)) + _bits(tmask(core, right))
 

@@ -1,37 +1,38 @@
-import math
 from concourse.bass import DstId, RemoteDMATransfer
 from concourse.mybir import AluOpType, AxisListType, ActivationFunctionType
 
 W = 256
 BL = 12
-SH = BL + 6
+Q = BL // 2
 SCRATCH = {
     "U": ("sbuf", [128, 272], "float32"),
     "B": ("sbuf", [128, 256], "float32"),
     "U9": ("sbuf", [128, 260], "float32"),
     "B4": ("sbuf", [128, 260], "float32"),
     "G": ("sbuf", [128, 260], "float32"),
-    "SQ": ("sbuf", [128, 256], "float32"),
-    "SQ2": ("sbuf", [128, 64], "float32"),
-    "SQ3": ("sbuf", [128, 64], "float32"),
+    "SQ": ("sbuf", [128, 260], "float32"),
     "Y": ("sbuf", [128, 256], "float32"),
+    "YR": ("sbuf", [128, 4], "float32"),
     "HB": ("sbuf", [128, 8], "float32"),
-    "HC": ("sbuf", [128, 4], "float32"),
+    "HC": ("sbuf", [128, 8], "float32"),
+    "HD": ("sbuf", [128, 8], "float32"),
     "L": ("sbuf", [128, 132], "float32"),
-    "E": ("sbuf", [128, 128], "float32"),
-    "EB": ("sbuf", [128, 64], "float32"),
-    "EM": ("sbuf", [128, 64], "float32"),
-    "EB2": ("sbuf", [128, 64], "float32"),
-    "EM2": ("sbuf", [128, 64], "float32"),
-    "QS": ("sbuf", [128, 4], "float32"),
+    "MK": ("sbuf", [128, 32], "float32"),
+    "XE": ("sbuf", [128, 32], "float32"),
+    "EE": ("sbuf", [128, 32], "float32"),
+    "ME": ("sbuf", [128, 32], "float32"),
+    "XL": ("sbuf", [128, 32], "float32"),
+    "EL": ("sbuf", [128, 32], "float32"),
+    "ML": ("sbuf", [128, 32], "float32"),
+    "J1": ("sbuf", [128, 32], "float32"),
+    "J2": ("sbuf", [128, 32], "float32"),
     "SO": ("sbuf", [128, 2], "float32"),
     "psW": ("psum", [128, 512], "float32"),
     "psH": ("psum", [128, 512], "float32"),
     "psY": ("psum", [128, 512], "float32"),
-    "psM": ("psum", [128, 512], "float32"),
 }
 SEMAPHORES = ["lu", "lb", "mz", "v", "ab", "pd", "ap", "gd", "pr", "halo", "ge", "ay", "yr", "pp", "red1", "red2",
-              "sent", "eb", "ae", "fb", "af", "sr", "st"]
+              "sent", "eb", "ae", "fb", "sr", "st"]
 
 
 def _bits(m):
@@ -85,23 +86,19 @@ def rank_program(g, core, T, topo):
         rid, pid, _ = topo.addr(dst)
         return DstId(rid=rid, pnc=pid)
 
-    U, B, U9, B4, G, Y, HB, HC, L, E, QS, SO = (
-        T.U, T.B, T.U9, T.B4, T.G, T.Y, T.HB, T.HC, T.L, T.E, T.QS, T.SO)
-    psW, psH, psY, psM = T.psW, T.psH, T.psY, T.psM
+    U, B, U9, B4, G, Y, YR, HB, HC, HD, L, MK, SO = (
+        T.U, T.B, T.U9, T.B4, T.G, T.Y, T.YR, T.HB, T.HC, T.HD, T.L, T.MK, T.SO)
+    psW, psH, psY = T.psW, T.psH, T.psY
 
-    def Mb(lo, hi):
-        return psM[:, lo:hi]
-
-    def M1(lo, hi):
-        return psM[:, 128 + lo:128 + hi]
-
-    own = BL * a
-    sc = 1.0 / math.sqrt(64.0 * n * W)
     near = list(range(1, 1 + (nch - 1) // 2))
     far = list(range(1 + (nch - 1) // 2, nch))
-    jl = 2 * len(far) + 1
-    lo_l, hi_l = BL, BL * jl + 6
-    lo_e, hi_e = BL * (jl + 1), BL * n + 6
+    mid = len(near)
+    own = CH * mid + BL * a
+    nbe = 2 * (mid + 1) - 1
+    we, wl = Q * nbe, Q * (n - nbe)
+
+    def place(dl):
+        return (mid - dl) % nch
 
     g.sync.dma_start(out=U[:, 8:264], in_=T.u[:, :]).then_inc(sem.lu, 16)
     ACT.dma_start(out=B[:, :], in_=T.b[:, :]).then_inc(sem.lb, 16)
@@ -141,7 +138,11 @@ def rank_program(g, core, T, topo):
     fill(U[:, 264:272], 0.0, s=sem.mz)
     fill(B4[:, 0:2], 0.0)
     fill(B4[:, 258:260], 0.0)
-    fill(L[:, own + 10:own + 12], 0.0)
+    fill(L[:, own + 9:own + 10], 0.5)
+    fill(L[:, own + 11:own + 12], 0.0)
+    fill(MK[:, :], 0.125)
+    vwait()
+    fill(MK[:, 4:32:Q], 0.0)
 
     ACT.wait_ge(sem.lu, 16)
     ACT.wait_ge(sem.mz, 2)
@@ -149,9 +150,10 @@ def rank_program(g, core, T, topo):
     ACT.wait_ge(sem.lb, 16)
     ACT.activation(out=B4[:, 2:258], in_=B[:, :], func=COPY, scale=4.0).then_inc(sem.ab, 1)
     ACT.wait_ge(sem.gd, 1)
-    ACT.activation(out=L[:, own + 6:own + 10], in_=G[:, 0:4], func=COPY).then_inc(sem.pr, 1)
-    ACT.activation(out=T.SQ[:, 0:252], in_=G[:, 4:256], func=SQUARE, scale=sc,
-                   accum_out=L[:, own + 4:own + 5]).then_inc(sem.pr, 1)
+    ACT.activation(out=L[:, own + 1:own + 8:2], in_=G[:, 0:4], func=COPY).then_inc(sem.pr, 1)
+    ACT.activation(out=T.SQ[:, 0:260], in_=G[:, 0:260], func=SQUARE,
+                   accum_out=L[:, own + 8:own + 9]).then_inc(sem.pr, 1)
+    ACT.activation(out=psY[:, 0:W], in_=G[:, 2:258], func=COPY, scale=0.125).then_inc(sem.ay, 1)
 
     V.wait_ge(sem.lu, 16)
     V.wait_ge(sem.mz, 2)
@@ -163,30 +165,20 @@ def rank_program(g, core, T, topo):
     V.wait_ge(sem.ab, 1)
     tt(G[:, 0:260], psH[:, 0:260], B4[:, :], ADD, s=sem.gd)
     V.wait_ge(sem.gd, 1)
-    red(L[:, own + 5:own + 6], G[:, 4:256], MAX, ab=True, dep=False, s=sem.pr)
-    cp(L[:, own:own + 4], G[:, 256:260], dep=False, s=sem.pr)
+    red(L[:, own + 10:own + 11], G[:, 4:256], MAX, ab=True, dep=False, s=sem.pr)
+    cp(L[:, own:own + 8:2], G[:, 256:260], dep=False, s=sem.pr)
 
-    fill(psM[:, 0:256], 0.0)
-    fill(E[:, hi_l:hi_l + 6], 0.0)
-    fill(E[:, lo_e + BL * (n - jl - 1) - 6:lo_e + BL * (n - jl - 1)], 0.0)
-    vwait()
-    for m in range(4):
-        fill(psM[:, m:hi_e:BL], sc)
-        fill(psM[:, 128 + m:128 + hi_e:BL], 0.125)
-    fill(psM[:, 128 + 5:128 + hi_e:BL], 0.125)
-    fill(psM[:, 128 + hi_l:128 + hi_l + 1], 1.0)
-
-    left, right = cores[(rank - 1) % n], cores[(rank + 1) % n]
-    V.wait_ge(sem.pr, 4)
-    V.wait_ge(sem.halo, _bits(tmask(left, core)) + _bits(tmask(right, core)))
-    tt(HC[:, 0:2], HB[:, 0:2], HB[:, 1:3], ADD, dep=False)
-    tt(HC[:, 2:4], HB[:, 5:7], HB[:, 6:8], ADD, dep=False)
-    tt(G[:, 2:4], G[:, 2:4], HC[:, 0:2], ADD, s=sem.ge)
-    tt(G[:, 256:258], G[:, 256:258], HC[:, 2:4], ADD, dep=False, s=sem.ge)
-    ACT.wait_ge(sem.ge, 2)
-    ACT.activation(out=psY[:, 0:W], in_=G[:, 2:258], func=COPY, scale=0.125).then_inc(sem.ay, 1)
     V.wait_ge(sem.ay, 1)
     tt(Y[:, :], psY[:, 0:W], U[:, 8:264], ADD, dep=False, s=sem.yr)
+
+    left, right = cores[(rank - 1) % n], cores[(rank + 1) % n]
+    V.wait_ge(sem.yr, 1)
+    V.wait_ge(sem.halo, _bits(tmask(left, core)) + _bits(tmask(right, core)))
+    tt(HC[:, 0:7], HB[:, 0:7], HB[:, 1:8], ADD, dep=False)
+    vwait()
+    done(V.tensor_scalar(out=HD[:, 0:7], in0=HC[:, 0:7], scalar1=0.125, scalar2=None, op0=MUL), None)
+    tt(YR[:, 0:2], Y[:, 0:2], HD[:, 0:2], ADD, s=sem.ge)
+    tt(YR[:, 2:4], Y[:, 254:256], HD[:, 5:7], ADD, dep=False, s=sem.ge)
 
     g.wait_ge(sem.lu, 16)
     g.wait_ge(sem.mz, 2)
@@ -198,60 +190,58 @@ def rank_program(g, core, T, topo):
     ], local_sem=sem.sent)
     nsent = _bits(tmask(core, left)) + _bits(tmask(core, right))
 
-    d1 = [(t, nch - dl) for dl in near for t in on_chip[chips[(k + dl) % nch]]]
-    d2 = [(same_die(chips[(k + dl) % nch], core), nch - dl) for dl in far]
+    d1 = [(t, place(dl)) for dl in near for t in on_chip[chips[(k + dl) % nch]]]
+    d2 = [(same_die(chips[(k + dl) % nch], core), place(dl)) for dl in far]
     m1, m2 = tmask(core, d1[0][0]), tmask(core, d2[0][0])
     g.wait_ge(sem.pr, 4)
     g.remote_dma_fused([
         RemoteDMATransfer(dst_ids=[did(mate)], dma_engine_mask=tmask(core, mate), remote_sem=sem.pp,
                           srcs=[L[:, own:own + BL]], dsts=[L[:, own:own + BL]], alu_op=0),
         RemoteDMATransfer(dst_ids=[did(t) for t, sl in d1], dma_engine_mask=m1, remote_sem=sem.red1,
-                          srcs=[L[:, own:own + BL]], dsts=[L[:, CH * sl + own:CH * sl + own + BL] for t, sl in d1],
-                          alu_op=0),
+                          srcs=[L[:, own:own + BL]],
+                          dsts=[L[:, CH * sl + BL * a:CH * sl + BL * a + BL] for t, sl in d1], alu_op=0),
     ], local_sem=sem.sent)
     nsent += _bits(tmask(core, mate)) + _bits(m1)
     g.wait_ge(sem.pp, _bits(tmask(mate, core)))
     g.remote_dma_fused([
         RemoteDMATransfer(dst_ids=[did(t) for t, sl in d2], dma_engine_mask=m2, remote_sem=sem.red2,
-                          srcs=[L[:, 0:CH]], dsts=[L[:, CH * sl:CH * sl + CH] for t, sl in d2], alu_op=0),
+                          srcs=[L[:, CH * mid:CH * mid + CH]], dsts=[L[:, CH * sl:CH * sl + CH] for t, sl in d2],
+                          alu_op=0),
     ], local_sem=sem.sent)
     nsent += _bits(m2)
     g.wait_ge(sem.sent, nsent)
 
     n1 = sum(_bits(tmask(t, core)) for dl in near for t in on_chip[chips[(k - dl) % nch]])
     n2 = sum(_bits(tmask(same_die(chips[(k - dl) % nch], core), core)) for dl in far)
-    we = hi_e - lo_e
+    ev_e, od_e = L[:, 0:BL * nbe:2], L[:, BL + 1:BL * (nbe + 1):2]
+    ev_l, od_l = L[:, BL * nbe:BL * n:2], L[:, BL * (nbe + 1) + 1:BL * (n + 1):2]
+    V.wait_ge(sem.pr, 4)
     V.wait_ge(sem.pp, _bits(tmask(mate, core)))
     V.wait_ge(sem.red1, n1)
+    tt(T.XE[:, 0:we], ev_e, od_e, MUL, s=sem.eb)
+    tt(T.EE[:, 0:we], ev_e, od_e, ADD, dep=False)
     cp(L[:, BL * n:BL * n + BL], L[:, 0:BL], dep=False)
-    tt(E[:, BL * n:hi_e], L[:, 0:6], L[:, SH:SH + 6], ADD, dep=False)
-    tt(E[:, lo_e:BL * n - 6], L[:, lo_e:BL * n - 6], L[:, lo_e + SH:BL * n - 6 + SH], ADD)
-    tt(T.EB2[:, 0:we], E[:, lo_e:hi_e], Mb(lo_e, hi_e), MUL, s=sem.eb)
-    tt(T.EM2[:, 0:we], E[:, lo_e:hi_e], M1(lo_e, hi_e), MUL, dep=False)
-    red(QS[:, 0:1], E[:, lo_e + 4:hi_e:BL], ADD, dep=False)
+    tt(T.ME[:, 0:we], T.EE[:, 0:we], MK[:, 0:we], MUL)
+    red(T.ML[:, wl:wl + 1], T.ME[:, 0:we], MAX, ab=True)
     ACT.wait_ge(sem.eb, 1)
-    ACT.activation(out=T.SQ2[:, 0:we], in_=T.EB2[:, 0:we], func=SQUARE,
-                   accum_out=QS[:, 1:2]).then_inc(sem.ae, 1)
-    red(E[:, hi_l:hi_l + 1], T.EM2[:, 0:we], MAX, ab=True)
-    V.wait_ge(sem.eb, 1)
-    V.wait_ge(sem.ae, 1)
-    tt(E[:, lo_e + 4:lo_e + 5], QS[:, 0:1], QS[:, 1:2], ADD)
+    ACT.activation(out=T.J1[:, 0:we], in_=T.XE[:, 0:we], func=COPY,
+                   accum_out=T.XL[:, wl:wl + 1]).then_inc(sem.ae, 1)
 
-    wl = hi_l - lo_l
     V.wait_ge(sem.red2, n2)
-    tt(E[:, lo_l:hi_l], L[:, lo_l:hi_l], L[:, lo_l + SH:hi_l + SH], ADD, dep=False)
-    tt(T.EB[:, 0:wl], E[:, lo_l:hi_l], Mb(lo_l, hi_l), MUL, s=sem.fb)
-    tt(T.EM[:, 0:wl + 6], E[:, lo_l:hi_l + 6], M1(lo_l, hi_l + 6), MUL, dep=False)
-    red(QS[:, 2:3], E[:, lo_l + 4:lo_e + 5:BL], ADD, dep=False)
+    tt(T.XL[:, 0:wl], ev_l, od_l, MUL, s=sem.fb)
+    tt(T.EL[:, 0:wl], ev_l, od_l, ADD, dep=False)
+    tt(T.ML[:, 0:wl], T.EL[:, 0:wl], MK[:, 0:wl], MUL)
+    red(SO[:, 1:2], T.ML[:, 0:wl + 1], MAX, ab=True, s=sem.sr)
+    ACT.wait_ge(sem.ae, 1)
     ACT.wait_ge(sem.fb, 1)
-    ACT.activation(out=T.SQ3[:, 0:wl], in_=T.EB[:, 0:wl], func=SQUARE,
-                   accum_out=QS[:, 3:4]).then_inc(sem.af, 1)
-    red(SO[:, 1:2], T.EM[:, 0:wl + 6], MAX, ab=True)
-    V.wait_ge(sem.af, 1)
-    tt(SO[:, 0:1], QS[:, 2:3], QS[:, 3:4], ADD, s=sem.sr)
+    ACT.activation(out=T.J2[:, 0:wl + 1], in_=T.XL[:, 0:wl + 1], func=COPY, scale=2.0 / (64.0 * n * W),
+                   accum_out=SO[:, 0:1]).then_inc(sem.sr, 1)
 
     g.sync.wait_ge(sem.yr, 1)
-    g.sync.dma_start(out=T.y[:, :], in_=Y[:, :]).then_inc(sem.st, 16)
-    g.sync.wait_ge(sem.sr, 1)
+    g.sync.dma_start(out=T.y[:, 2:254], in_=Y[:, 2:254]).then_inc(sem.st, 16)
+    g.sync.wait_ge(sem.ge, 2)
+    g.sync.dma_start(out=T.y[:, 0:2], in_=YR[:, 0:2]).then_inc(sem.st, 16)
+    g.sync.dma_start(out=T.y[:, 254:256], in_=YR[:, 2:4]).then_inc(sem.st, 16)
+    g.sync.wait_ge(sem.sr, 2)
     g.sync.dma_start(out=T.s[:, :], in_=SO[:, :]).then_inc(sem.st, 16)
-    g.sync.wait_ge(sem.st, 32)
+    g.sync.wait_ge(sem.st, 64)

from concourse.bass import DstId, RemoteDMATransfer
from concourse.mybir import AluOpType, AxisListType, ActivationFunctionType

W = 256
BL = 12
Q = BL // 2
SCRATCH = {
    "U": ("sbuf", [128, 272], "float32"),
    "B": ("sbuf", [128, 256], "float32"),
    "U9": ("sbuf", [128, 260], "float32"),
    "B4": ("sbuf", [128, 260], "float32"),
    "G": ("sbuf", [128, 260], "float32"),
    "SQ": ("sbuf", [128, 260], "float32"),
    "Y": ("sbuf", [128, 256], "float32"),
    "YR": ("sbuf", [128, 4], "float32"),
    "HB": ("sbuf", [128, 8], "float32"),
    "HC": ("sbuf", [128, 8], "float32"),
    "HD": ("sbuf", [128, 8], "float32"),
    "L": ("sbuf", [128, 132], "float32"),
    "MK": ("sbuf", [128, 32], "float32"),
    "XE": ("sbuf", [128, 32], "float32"),
    "EE": ("sbuf", [128, 32], "float32"),
    "ME": ("sbuf", [128, 32], "float32"),
    "XL": ("sbuf", [128, 32], "float32"),
    "EL": ("sbuf", [128, 32], "float32"),
    "ML": ("sbuf", [128, 32], "float32"),
    "J1": ("sbuf", [128, 32], "float32"),
    "J2": ("sbuf", [128, 32], "float32"),
    "SO": ("sbuf", [128, 2], "float32"),
    "psW": ("psum", [128, 512], "float32"),
    "psH": ("psum", [128, 512], "float32"),
    "psY": ("psum", [128, 512], "float32"),
}
SEMAPHORES = ["lu", "lb", "mz", "v", "ab", "pd", "ap", "gd", "pr", "halo", "ge", "ay", "yr", "pp", "red1", "red2",
              "sent", "eb", "ae", "fb", "sr", "st"]


def _bits(m):
    return bin(m).count("1")


def _take(m, n):
    out, k = 0, 0
    while n > 0:
        if (m >> k) & 1:
            out |= 1 << k
            n -= 1
        k += 1
    return out


def rank_program(g, core, T, topo):
    rank = T.rank_of(core)
    if rank is None:
        return
    cores = list(T.cores)
    n = len(cores)
    sem = T.sem
    V, ACT = g.vector, g.scalar
    ADD, SUB, MUL, MAX = AluOpType.add, AluOpType.subtract, AluOpType.mult, AluOpType.max
    COPY, SQUARE = ActivationFunctionType.Copy, ActivationFunctionType.Square
    X = AxisListType.X

    chips = []
    for c in cores:
        if topo.chip(c) not in chips:
            chips.append(topo.chip(c))
    on_chip = {ch: [c for c in cores if topo.chip(c) == ch] for ch in chips}
    nch = len(chips)
    k = chips.index(topo.chip(core))
    a = on_chip[chips[k]].index(core)
    mate = on_chip[chips[k]][1 - a]
    CH = 2 * BL

    def same_die(ch, c):
        return [t for t in on_chip[ch] if topo.die(t) == topo.die(c)][0]

    def tmask(src, dst):
        if topo.chip(src) != topo.chip(dst):
            return topo.mask(src, dst)
        far_core = [c for c in cores if topo.chip(c) != topo.chip(src)][0]
        return _take(topo.mask(src, dst) & ~topo.mask(src, far_core), 4)

    def did(dst):
        assert topo.may_write(core, dst)
        rid, pid, _ = topo.addr(dst)
        return DstId(rid=rid, pnc=pid)

    U, B, U9, B4, G, Y, YR, HB, HC, HD, L, MK, SO = (
        T.U, T.B, T.U9, T.B4, T.G, T.Y, T.YR, T.HB, T.HC, T.HD, T.L, T.MK, T.SO)
    psW, psH, psY = T.psW, T.psH, T.psY

    near = list(range(1, 1 + (nch - 1) // 2))
    far = list(range(1 + (nch - 1) // 2, nch))
    mid = len(near)
    own = CH * mid + BL * a
    nbe = 2 * (mid + 1) - 1
    we, wl = Q * nbe, Q * (n - nbe)

    def place(dl):
        return (mid - dl) % nch

    g.sync.dma_start(out=U[:, 8:264], in_=T.u[:, :]).then_inc(sem.lu, 16)
    ACT.dma_start(out=B[:, :], in_=T.b[:, :]).then_inc(sem.lb, 16)

    cnt = [0]

    def vwait():
        if cnt[0]:
            V.wait_ge(sem.v, cnt[0])

    def done(ins, s):
        if s is None:
            ins.then_inc(sem.v, 1)
            cnt[0] += 1
        else:
            ins.then_inc(s, 1)

    def fill(ap, val, s=None):
        done(V.memset(ap, val), s)

    def tt(out, x, y, op, dep=True, s=None):
        if dep:
            vwait()
        done(V.tensor_tensor(out=out, in0=x, in1=y, op=op), s)

    def cp(out, x, dep=True, s=None):
        if dep:
            vwait()
        done(V.tensor_copy(out=out, in_=x), s)

    def red(out, x, op, ab=False, dep=True, s=None):
        if dep:
            vwait()
        done(V.tensor_reduce(out=out, in_=x, axis=X, op=op, apply_absolute_value=ab), s)

    fill(U[:, 0:8], 0.0, s=sem.mz)
    fill(U[:, 264:272], 0.0, s=sem.mz)
    fill(B4[:, 0:2], 0.0)
    fill(B4[:, 258:260], 0.0)
    fill(L[:, own + 9:own + 10], 0.5)
    fill(L[:, own + 11:own + 12], 0.0)
    fill(MK[:, :], 0.125)
    vwait()
    fill(MK[:, 4:32:Q], 0.0)

    ACT.wait_ge(sem.lu, 16)
    ACT.wait_ge(sem.mz, 2)
    ACT.activation(out=U9[:, :], in_=U[:, 6:266], func=COPY, scale=9.0).then_inc(sem.ap, 1)
    ACT.wait_ge(sem.lb, 16)
    ACT.activation(out=B4[:, 2:258], in_=B[:, :], func=COPY, scale=4.0).then_inc(sem.ab, 1)
    ACT.wait_ge(sem.gd, 1)
    ACT.activation(out=L[:, own + 1:own + 8:2], in_=G[:, 0:4], func=COPY).then_inc(sem.pr, 1)
    ACT.activation(out=T.SQ[:, 0:260], in_=G[:, 0:260], func=SQUARE,
                   accum_out=L[:, own + 8:own + 9]).then_inc(sem.pr, 1)
    ACT.activation(out=psY[:, 0:W], in_=G[:, 2:258], func=COPY, scale=0.125).then_inc(sem.ay, 1)

    V.wait_ge(sem.lu, 16)
    V.wait_ge(sem.mz, 2)
    V.tensor_tensor_scan(out=psW[:, 0:260], data0=U[:, 8:268], data1=U[:, 3:263], initial=0.0,
                         op0=ADD, op1=SUB).then_inc(sem.pd, 1)
    V.wait_ge(sem.pd, 1)
    V.wait_ge(sem.ap, 1)
    tt(psH[:, 0:260], psW[:, 0:260], U9[:, :], SUB, dep=False)
    V.wait_ge(sem.ab, 1)
    tt(G[:, 0:260], psH[:, 0:260], B4[:, :], ADD, s=sem.gd)
    V.wait_ge(sem.gd, 1)
    red(L[:, own + 10:own + 11], G[:, 4:256], MAX, ab=True, dep=False, s=sem.pr)
    cp(L[:, own:own + 8:2], G[:, 256:260], dep=False, s=sem.pr)

    V.wait_ge(sem.ay, 1)
    tt(Y[:, :], psY[:, 0:W], U[:, 8:264], ADD, dep=False, s=sem.yr)

    left, right = cores[(rank - 1) % n], cores[(rank + 1) % n]
    V.wait_ge(sem.yr, 1)
    V.wait_ge(sem.halo, _bits(tmask(left, core)) + _bits(tmask(right, core)))
    tt(HC[:, 0:7], HB[:, 0:7], HB[:, 1:8], ADD, dep=False)
    vwait()
    done(V.tensor_scalar(out=HD[:, 0:7], in0=HC[:, 0:7], scalar1=0.125, scalar2=None, op0=MUL), None)
    tt(YR[:, 0:2], Y[:, 0:2], HD[:, 0:2], ADD, s=sem.ge)
    tt(YR[:, 2:4], Y[:, 254:256], HD[:, 5:7], ADD, dep=False, s=sem.ge)

    g.wait_ge(sem.lu, 16)
    g.wait_ge(sem.mz, 2)
    g.remote_dma_fused([
        RemoteDMATransfer(dst_ids=[did(left)], dma_engine_mask=tmask(core, left), remote_sem=sem.halo,
                          srcs=[U[:, 6:10]], dsts=[HB[:, 4:8]], alu_op=0),
        RemoteDMATransfer(dst_ids=[did(right)], dma_engine_mask=tmask(core, right), remote_sem=sem.halo,
                          srcs=[U[:, 262:266]], dsts=[HB[:, 0:4]], alu_op=0),
    ], local_sem=sem.sent)
    nsent = _bits(tmask(core, left)) + _bits(tmask(core, right))

    d1 = [(t, place(dl)) for dl in near for t in on_chip[chips[(k + dl) % nch]]]
    d2 = [(same_die(chips[(k + dl) % nch], core), place(dl)) for dl in far]
    m1, m2 = tmask(core, d1[0][0]), tmask(core, d2[0][0])
    g.wait_ge(sem.pr, 4)
    g.remote_dma_fused([
        RemoteDMATransfer(dst_ids=[did(mate)], dma_engine_mask=tmask(core, mate), remote_sem=sem.pp,
                          srcs=[L[:, own:own + BL]], dsts=[L[:, own:own + BL]], alu_op=0),
        RemoteDMATransfer(dst_ids=[did(t) for t, sl in d1], dma_engine_mask=m1, remote_sem=sem.red1,
                          srcs=[L[:, own:own + BL]],
                          dsts=[L[:, CH * sl + BL * a:CH * sl + BL * a + BL] for t, sl in d1], alu_op=0),
    ], local_sem=sem.sent)
    nsent += _bits(tmask(core, mate)) + _bits(m1)
    g.wait_ge(sem.pp, _bits(tmask(mate, core)))
    g.remote_dma_fused([
        RemoteDMATransfer(dst_ids=[did(t) for t, sl in d2], dma_engine_mask=m2, remote_sem=sem.red2,
                          srcs=[L[:, CH * mid:CH * mid + CH]], dsts=[L[:, CH * sl:CH * sl + CH] for t, sl in d2],
                          alu_op=0),
    ], local_sem=sem.sent)
    nsent += _bits(m2)
    g.wait_ge(sem.sent, nsent)

    n1 = sum(_bits(tmask(t, core)) for dl in near for t in on_chip[chips[(k - dl) % nch]])
    n2 = sum(_bits(tmask(same_die(chips[(k - dl) % nch], core), core)) for dl in far)
    ev_e, od_e = L[:, 0:BL * nbe:2], L[:, BL + 1:BL * (nbe + 1):2]
    ev_l, od_l = L[:, BL * nbe:BL * n:2], L[:, BL * (nbe + 1) + 1:BL * (n + 1):2]
    V.wait_ge(sem.pr, 4)
    V.wait_ge(sem.pp, _bits(tmask(mate, core)))
    V.wait_ge(sem.red1, n1)
    tt(T.XE[:, 0:we], ev_e, od_e, MUL, s=sem.eb)
    tt(T.EE[:, 0:we], ev_e, od_e, ADD, dep=False)
    cp(L[:, BL * n:BL * n + BL], L[:, 0:BL], dep=False)
    tt(T.ME[:, 0:we], T.EE[:, 0:we], MK[:, 0:we], MUL)
    red(T.ML[:, wl:wl + 1], T.ME[:, 0:we], MAX, ab=True)
    ACT.wait_ge(sem.eb, 1)
    ACT.activation(out=T.J1[:, 0:we], in_=T.XE[:, 0:we], func=COPY,
                   accum_out=T.XL[:, wl:wl + 1]).then_inc(sem.ae, 1)

    V.wait_ge(sem.red2, n2)
    tt(T.XL[:, 0:wl], ev_l, od_l, MUL, s=sem.fb)
    tt(T.EL[:, 0:wl], ev_l, od_l, ADD, dep=False)
    tt(T.ML[:, 0:wl], T.EL[:, 0:wl], MK[:, 0:wl], MUL)
    red(SO[:, 1:2], T.ML[:, 0:wl + 1], MAX, ab=True, s=sem.sr)
    ACT.wait_ge(sem.ae, 1)
    ACT.wait_ge(sem.fb, 1)
    ACT.activation(out=T.J2[:, 0:wl + 1], in_=T.XL[:, 0:wl + 1], func=COPY, scale=2.0 / (64.0 * n * W),
                   accum_out=SO[:, 0:1]).then_inc(sem.sr, 1)

    g.sync.wait_ge(sem.yr, 1)
    g.sync.dma_start(out=T.y[:, 2:254], in_=Y[:, 2:254]).then_inc(sem.st, 16)
    g.sync.wait_ge(sem.ge, 2)
    g.sync.dma_start(out=T.y[:, 0:2], in_=YR[:, 0:2]).then_inc(sem.st, 16)
    g.sync.dma_start(out=T.y[:, 254:256], in_=YR[:, 2:4]).then_inc(sem.st, 16)
    g.sync.wait_ge(sem.sr, 2)
    g.sync.dma_start(out=T.s[:, :], in_=SO[:, :]).then_inc(sem.st, 16)
    g.sync.wait_ge(sem.st, 64)
